import numpy as np
import ml_dtypes


def mxq(x, axis, fmt="e4m3"):
    dtype, down = {"e4m3": (ml_dtypes.float8_e4m3fn, 7), "e5m2": (ml_dtypes.float8_e5m2, 14)}[fmt]
    v = np.moveaxis(np.asarray(x, np.float32).astype(ml_dtypes.bfloat16).astype(np.float64), axis, -1)
    blocks = v.reshape(v.shape[:-1] + (-1, 32))
    amax = np.abs(blocks).max(-1, keepdims=True)
    byte = np.maximum(np.where(amax > 0, np.frexp(amax)[1] - 1 + 127, 0) - down, 1)
    scale = np.exp2(byte - 127.0)
    codes = (blocks / scale).astype(np.float32).astype(dtype).astype(np.float64)
    return np.moveaxis((codes * scale).reshape(v.shape), -1, axis)


WIDE = False


def mx_kscale(k):
    if not WIDE:
        return np.ones(k)
    levels = np.array([10, -10, 5, -5, 0])
    if k % 512:
        return np.exp2(np.random.permutation(np.resize(levels, k // 32))).repeat(32)
    a = np.empty((k // 512, 16))
    for p in range(k // 512):
        a[p, :8] = np.random.permutation(np.resize(levels, 8))
        for g in range(8):
            far = levels[np.abs(levels - a[p, g]) >= 10]
            a[p, g + 8] = far[np.random.randint(len(far))]
    return np.exp2(a.ravel()).repeat(32)


BF16 = ml_dtypes.bfloat16


def bf(x):
    return np.asarray(x, np.float32).astype(BF16)


def f64(x):
    return np.asarray(x).astype(np.float64)


E2M1 = np.array([0.0, 0.5, 1.0, 1.5, 2.0, 3.0, 4.0, 6.0, -0.0, -0.5, -1.0, -1.5, -2.0, -3.0, -4.0, -6.0])


def pack_weight(w, fmt):
    k, n = w.shape
    w = f64(bf(w)).reshape(k // 32, 32, n)
    amax = np.abs(w).max(1)
    if fmt == "e4m3":
        byte = np.frexp(amax)[1] - 1 + 127 - 7
    else:
        mant, ex = np.frexp(amax / 6.0)
        byte = np.where(mant > 0.5, ex, ex - 1) + 127
    byte = np.clip(np.where(amax > 0, byte, 1), 1, 254)
    scaled = (w * np.exp2(127.0 - byte)[:, None, :]).reshape(k, n).astype(np.float32)
    by_word = np.ascontiguousarray(scaled.reshape(k // 512, 128, 4, n).transpose(0, 1, 3, 2))
    if fmt == "e4m3":
        words = by_word.astype(ml_dtypes.float8_e4m3fn).view(np.uint8)
    else:
        c = by_word.astype(ml_dtypes.float4_e2m1fn).view(np.uint8) & 0xF
        words = c[..., 0::2] | (c[..., 1::2] << 4)
    return np.ascontiguousarray(words), np.ascontiguousarray(byte.astype(np.uint8).reshape(k // 512, 16, n))


def unpack_weight(words, scales, fmt):
    g, p, n, _ = words.shape
    if fmt == "e4m3":
        vals = np.ascontiguousarray(words).view(ml_dtypes.float8_e4m3fn).astype(np.float64)
    else:
        nib = np.empty((g, p, n, 4), np.uint8)
        nib[..., 0::2] = words & 0xF
        nib[..., 1::2] = words >> 4
        vals = E2M1[nib]
    vals = vals * np.repeat(np.exp2(scales.astype(np.float64) - 127.0), 8, axis=1)[..., None]
    return vals.transpose(0, 1, 3, 2).reshape(g * 512, n)
def pack4(w):
    words, scales = pack_weight(w, "e2m1")
    return words.reshape(words.shape[0], 128, -1), scales


def unpack4(words, scales):
    return unpack_weight(words.reshape(words.shape[0], 128, -1, 2), scales, "e2m1")


M, R, C, K, N = 256, 64, 32, 4096, 1024
PAIR_NOISE = 0.3
BIAS_SCALE = 0.5


def setup_inputs():
    s = mx_kscale(K)
    adj = np.random.standard_normal((M, K)) * s
    soft = np.exp(np.random.standard_normal((3, R, C)))
    soft = soft / soft.sum(axis=2, keepdims=True)
    soft = soft / np.sqrt((soft ** 2).sum(axis=1, keepdims=True))
    pairs = []
    for h in soft:
        both = np.kron(h, h)
        both = both * np.exp(PAIR_NOISE * np.random.standard_normal((K, N)))
        pairs.append(both / s[:, None])
    base_words, base_scales = pack4(pairs[0])
    gate_words, gate_scales = pack_weight(pairs[1], "e4m3")
    return {"adj": bf(adj),
            "base_words": base_words, "base_scales": base_scales,
            "gate_words": gate_words, "gate_scales": gate_scales,
            "task": bf(pairs[2]),
            "bias": bf(BIAS_SCALE * np.random.standard_normal(N))}


def reference(adj, base_words, base_scales, gate_words, gate_scales, task, bias):
    a = mxq(f64(adj), 1, "e4m3")
    base = a @ unpack4(base_words, base_scales)
    gate = a @ unpack_weight(gate_words, gate_scales, "e4m3")
    own = a @ mxq(f64(task), 0, "e4m3")
    open_ = 1.0 / (1.0 + np.exp(-(gate + f64(bias))))
    return base * open_ + own

from contextlib import ExitStack

import concourse.mybir as mybir
from concourse.masks import make_identity

P = 128
M, K, N = 256, 4096, 1024
K_PASS = 512
GROUPS = K // K_PASS
H = 512

FLOPS = 3 * 2 * M * K * N

F32 = mybir.dt.float32
BF16 = mybir.dt.bfloat16
I32 = mybir.dt.int32
U32 = mybir.dt.uint32
U8 = mybir.dt.uint8
E4M3X4 = mybir.dt.float8_e4m3fn_x4
E2M1X4 = mybir.dt.float4_e2m1fn_x4
ADD = mybir.AluOpType.add
MULT = mybir.AluOpType.mult
SIGMOID = mybir.ActivationFunctionType.Sigmoid


def tile_diffpool_pair_coarsening_s10_kernel(
    tc, adj, base_words, base_scales, gate_words, gate_scales, task, bias, out
):
    nc = tc.nc
    with ExitStack() as ctx:
        keep = ctx.enter_context(tc.tile_pool(name="keep", bufs=1))
        work = ctx.enter_context(tc.tile_pool(name="work", bufs=3))
        psum = ctx.enter_context(tc.psum_pool(name="psum", bufs=1))
        ctx.enter_context(tc.manual_schedule())

        def kept(name, shape, dtype):
            return keep.tile(shape, dtype, name=name, tag=name, align_bytes=64)

        warm = kept("warm", [P, 1], F32)
        nc.vector.memset(warm[:], 0.0)
        warm_out = kept("warm_out", [P, 1], F32)
        nc.scalar.activation(out=warm_out[:], in_=warm[:], func=SIGMOID)
        ident = kept("ident", [P, P], F32)
        make_identity(nc, ident[:])
        gate_planes = [kept(f"gate_plane{i}", [P, N], U8) for i in range(2)]
        base_plane = kept("base_plane", [P, GROUPS * N], U8)
        bias_rows = kept("bias_rows", [P, P], BF16)
        nc.vector.memset(gate_planes[0][:].bitcast(I32), 0)
        nc.vector.memset(bias_rows[:], 0.0)
        nc.vector.memset(gate_planes[1][:].bitcast(I32), 0)
        nc.vector.memset(base_plane[:].bitcast(I32), 0)
        ident_bf = kept("ident_bf", [P, P], BF16)
        nc.vector.tensor_copy(out=ident_bf[:], in_=ident[:])

        def load_gate_scales(i):
            for q in range(4):
                nc.gpsimd.dma_start(
                    out=gate_planes[i][32 * q : 32 * q + 16, :].bitcast(I32),
                    in_=gate_scales[4 * i : 4 * i + 4, 4 * q : 4 * q + 4, :].bitcast(I32),
                )

        load_gate_scales(0)
        nc.gpsimd.dma_start(out=bias_rows[0:8, :], in_=bias.rearrange("(c p) -> c p", p=P))
        load_gate_scales(1)
        base_plane_3d = base_plane[:].rearrange("p (g n) -> p g n", n=N)
        for q in range(4):
            nc.gpsimd.dma_start(
                out=base_plane_3d[32 * q : 32 * q + 4, :, :].bitcast(I32),
                in_=base_scales[:, 4 * q : 4 * q + 4, :].rearrange("g r n -> r g n").bitcast(I32),
            )

        adj_tiles = {}
        gate_tiles = {}
        base_tiles = {}
        task_tiles = {}

        def load_adj(c):
            t = kept(f"adj{c}", [P, 2, 1024], BF16)
            nc.sync.dma_start(out=t[:], in_=adj[:, 1024 * c : 1024 * (c + 1)].rearrange("(b p) k -> p b k", p=P))
            adj_tiles[c] = t

        def load_gate(i):
            t = kept(f"gate{i}", [P, 2, 4 * N], U8)
            nc.sync.dma_start(
                out=t[:].bitcast(I32),
                in_=gate_words[2 * i : 2 * i + 2].rearrange("g p n t -> p g (n t)").bitcast(I32),
            )
            gate_tiles[i] = t

        def load_base(i):
            t = kept(f"base{i}", [P, 2, 2 * N], U8)
            nc.sync.dma_start(
                out=t[:].bitcast(I32), in_=base_words[2 * i : 2 * i + 2].rearrange("g p b -> p g b").bitcast(I32)
            )
            base_tiles[i] = t

        def load_task(g, h0=0, h1=N):
            t = kept(f"task{g}_{h0}", [P, 4, h1 - h0], BF16)
            nc.sync.dma_start(
                out=t[:], in_=task[K_PASS * g : K_PASS * (g + 1), h0:h1].rearrange("(p j) n -> p j n", j=4)
            )
            for h in range(h0 // H, h1 // H):
                task_tiles[g, h] = t[:, :, H * h - h0 : H * h - h0 + H]

        for c in range(4):
            load_adj(c)
        for i in range(4):
            load_gate(i)
            load_task(i)
        for i in range(3):
            load_base(i)
            load_task(4 + i)
        load_base(3)
        load_task(7, 0, H)
        load_task(7, H, N)

        def bank(name, shape, dtype, tag):
            return psum.tile(shape, dtype, name=name, tag=tag)

        a_codes = []
        a_scales = []

        def adj_group(g):
            words = adj_tiles[g // 2][:].bitcast(F32)
            w0 = 256 * (g % 2)
            xt = bank("xt", [P, 2, 256], F32, f"own{g % 4}")
            for b in range(2):
                for u in range(2):
                    nc.tensor.transpose(
                        xt[:, u, P * b : P * (b + 1)], words[:, b, w0 + u : w0 + 256 : 2], ident[:]
                    )
            grouped = work.tile([P, 256, 4], BF16, name="a_grouped", tag="a_grouped", align_bytes=64)
            nc.scalar.copy(out=grouped[:].bitcast(F32), in_=xt[:].rearrange("p u r -> p r u"))
            codes = kept(f"a_codes{g}", [P, 256], U32)
            scales = kept(f"a_scales{g}", [P, 256], U8)
            nc.vector.quantize_mx(
                out=codes[:].bitcast(E4M3X4), scales=scales[:], in_=grouped[:].rearrange("p r t -> p (r t)")
            )
            a_codes.append(codes)
            a_scales.append(scales)

        for g in range(GROUPS):
            adj_group(g)

        turned = bank("turned", [P, P], BF16, "own0")
        nc.tensor.transpose(turned[:], bias_rows[:], ident_bf[:])
        bias_cols = kept("bias_cols", [P, P], BF16)
        nc.scalar.copy(out=bias_cols[:], in_=turned[:])
        spread = bank("spread", [P, N], BF16, "own1")
        for c in range(8):
            nc.tensor.transpose(
                spread[:, P * c : P * (c + 1)], bias_cols[:, c : c + 1].to_broadcast([P, P]), ident_bf[:]
            )
        bias_all = kept("bias_all", [P, N], BF16)
        nc.scalar.copy(out=bias_all[:], in_=spread[:])

        gate_ps = {}
        base_ps = {}
        own_ps = {}
        HM = [(h, m) for h in range(2) for m in range(2)]
        t_codes = {}

        def mx(acc, g, m, rhs, rhs_scale):
            nc.tensor.matmul_mx(
                out=acc[:],
                lhsT=a_codes[g][:, P * m : P * (m + 1)].bitcast(E4M3X4),
                lhsT_scale=a_scales[g][:, P * m : P * (m + 1)],
                rhs=rhs,
                rhs_scale=rhs_scale,
                start=(g == 0),
                stop=(g == GROUPS - 1),
            )

        def gate_pass(g, h, m):
            if g == 0:
                gate_ps[h, m] = bank("gate_ps", [P, H], F32, f"wt{2 * h + m}")
            words = gate_tiles[g // 2][:, g % 2, 4 * H * h : 4 * H * (h + 1)]
            plane = gate_planes[g // 4][4 * (g % 4) : P, H * h : H * (h + 1)]
            mx(gate_ps[h, m], g, m, words.bitcast(E4M3X4), plane)

        def base_pass(g, h, m):
            if g == 0:
                base_ps[h, m] = bank("base_ps", [P, H], F32, f"wt{2 * h + m}")
            words = base_tiles[g // 2][:, g % 2, 2 * H * h : 2 * H * (h + 1)]
            plane = base_plane[:, N * g + H * h : N * g + H * (h + 1)]
            mx(base_ps[h, m], g, m, words.bitcast(E2M1X4), plane)

        def own_pass(g, h, m):
            if g == 0:
                own_ps[h, m] = bank("own_ps", [P, H], F32, f"own{2 * h + m}")
            codes, scales = t_codes[g, h]
            mx(own_ps[h, m], g, m, codes[:].bitcast(E4M3X4), scales[:])

        def run(one_pass, groups):
            for h, m in HM:
                for g in groups:
                    one_pass(g, h, m)

        t_grouped = {}

        def group_tile(g, h):
            t_grouped[g, h] = work.tile([P, H, 4], BF16, name="t_grouped", tag=f"t_grouped{h}", align_bytes=64)

        def interleave(copy, g, h, c0, c1):
            dst = t_grouped[g, h][:, c0:c1, :].rearrange("p (c i) t -> p c t i", i=4)
            src = task_tiles[g, h][:, :, c0:c1].rearrange("p t (c i) -> p c t i", i=4)
            copy(out=dst, in_=src)

        def quantize(g, h):
            codes = work.tile([P, H], U32, name="t_codes", tag=f"t_codes{h}", align_bytes=64)
            scales = work.tile([P, H], U8, name="t_scales", tag=f"t_scales{h}", align_bytes=64)
            nc.vector.quantize_mx(
                out=codes[:].bitcast(E4M3X4), scales=scales[:], in_=t_grouped[g, h][:].rearrange("p n t -> p (n t)")
            )
            t_codes[g, h] = (codes, scales)

        def task_copies(g):
            group_tile(g, 0)
            group_tile(g, 1)
            interleave(nc.vector.tensor_copy, g, 0, 0, H)
            interleave(nc.scalar.copy, g, 1, 0, H)

        def task_group(g):
            task_copies(g)
            quantize(g, 0)
            quantize(g, 1)

        sums = {}
        opens = {}
        prods = {}

        def f32_tile(name, h, m):
            return kept(f"{name}{h}{m}", [P, H], F32)

        def add_bias(h, m):
            sums[h, m] = f32_tile("sum", h, m)
            nc.vector.tensor_tensor(
                out=sums[h, m][:], in0=gate_ps[h, m][:], in1=bias_all[:, H * h : H * (h + 1)], op=ADD
            )

        def sigmoid(h, m):
            opens[h, m] = f32_tile("open", h, m)
            nc.scalar.activation(out=opens[h, m][:], in_=sums[h, m][:], func=SIGMOID)

        def multiply(h, m):
            prods[h, m] = f32_tile("prod", h, m)
            nc.vector.tensor_tensor(out=prods[h, m][:], in0=base_ps[h, m][:], in1=opens[h, m][:], op=MULT)

        def finish(h, m):
            res = f32_tile("res", h, m)
            nc.vector.tensor_tensor(out=res[:], in0=own_ps[h, m][:], in1=prods[h, m][:], op=ADD)
            nc.sync.dma_start(out=out[P * m : P * (m + 1), H * h : H * (h + 1)], in_=res[:])

        run(gate_pass, (0, 1))
        for i in range(3):
            task_group(i)
            run(gate_pass, (2 * i + 2, 2 * i + 3))
            run(own_pass, (i,))
        task_copies(3)
        for h, m in HM:
            add_bias(h, m)
            sigmoid(h, m)
        quantize(3, 0)
        quantize(3, 1)
        for i in range(3):
            run(base_pass, (2 * i, 2 * i + 1))
            run(own_pass, (3 + i,))
            task_group(4 + i)
        run(base_pass, (6, 7))
        run(own_pass, (6,))

        V_LAST = 192
        for h in range(2):
            group_tile(7, h)
            interleave(nc.vector.tensor_copy, 7, h, 0, V_LAST)
            interleave(nc.scalar.copy, 7, h, V_LAST, H)
            multiply(0, h)
            quantize(7, h)
            for m in range(2):
                own_pass(7, h, m)
        multiply(1, 0)
        finish(0, 0)
        multiply(1, 1)
        finish(0, 1)
        finish(1, 0)
        finish(1, 1)
